import numpy as np
import ml_dtypes


def mxq(x, axis, fmt="e4m3"):
    dtype, down = {"e4m3": (ml_dtypes.float8_e4m3fn, 7), "e5m2": (ml_dtypes.float8_e5m2, 14)}[fmt]
    v = np.moveaxis(np.asarray(x, np.float32).astype(ml_dtypes.bfloat16).astype(np.float64), axis, -1)
    blocks = v.reshape(v.shape[:-1] + (-1, 32))
    amax = np.abs(blocks).max(-1, keepdims=True)
    byte = np.maximum(np.where(amax > 0, np.frexp(amax)[1] - 1 + 127, 0) - down, 1)
    scale = np.exp2(byte - 127.0)
    codes = (blocks / scale).astype(np.float32).astype(dtype).astype(np.float64)
    return np.moveaxis((codes * scale).reshape(v.shape), -1, axis)


WIDE = False


def mx_kscale(k):
    if not WIDE:
        return np.ones(k)
    levels = np.array([30, -30])
    if k % 512:
        return np.exp2(np.random.permutation(np.resize(levels, k // 32))).repeat(32)
    a = np.empty((k // 512, 16))
    for p in range(k // 512):
        a[p, :8] = np.random.permutation(np.resize(levels, 8))
        for g in range(8):
            far = levels[np.abs(levels - a[p, g]) >= 10]
            a[p, g + 8] = far[np.random.randint(len(far))]
    return np.exp2(a.ravel()).repeat(32)


def f64(x):
    return np.asarray(x).astype(np.float64)


def striped(idx):
    return np.tile(np.asarray(idx).reshape(-1, 16).T, (8, 1)).astype(np.uint16)


def unstriped(offs):
    return offs[:16].T.reshape(-1).astype(np.int64)


E2M1 = np.array([0.0, 0.5, 1.0, 1.5, 2.0, 3.0, 4.0, 6.0, -0.0, -0.5, -1.0, -1.5, -2.0, -3.0, -4.0, -6.0])


def pack_weight(w, fmt):
    k, n = w.shape
    w = f64(np.asarray(w, np.float32).astype(ml_dtypes.bfloat16)).reshape(k // 32, 32, n)
    amax = np.abs(w).max(1)
    if fmt in ("e4m3", "e5m2"):
        byte = np.frexp(amax)[1] - 1 + 127 - (7 if fmt == "e4m3" else 14)
    else:
        mant, ex = np.frexp(amax / 6.0)
        byte = np.where(mant > 0.5, ex, ex - 1) + 127
    byte = np.clip(np.where(amax > 0, byte, 1), 1, 254)
    scaled = (w * np.exp2(127.0 - byte)[:, None, :]).reshape(k, n).astype(np.float32)
    by_word = np.ascontiguousarray(scaled.reshape(k // 512, 128, 4, n).transpose(0, 1, 3, 2))
    if fmt in ("e4m3", "e5m2"):
        words = by_word.astype(ml_dtypes.float8_e4m3fn if fmt == "e4m3" else ml_dtypes.float8_e5m2).view(np.uint8)
    else:
        c = by_word.astype(ml_dtypes.float4_e2m1fn).view(np.uint8) & 0xF
        words = (c[..., 0::2] | (c[..., 1::2] << 4)).reshape(k // 512, 128, 2 * n)
    return np.ascontiguousarray(words), np.ascontiguousarray(byte.astype(np.uint8).reshape(k // 512, 16, n))


def unpack_weight(words, scales, fmt):
    g, _, n = scales.shape
    words = np.ascontiguousarray(words).reshape(g, 128, n, -1)
    if fmt in ("e4m3", "e5m2"):
        vals = words.view(ml_dtypes.float8_e4m3fn if fmt == "e4m3" else ml_dtypes.float8_e5m2).astype(np.float64)
    else:
        nib = np.empty((g, 128, n, 4), np.uint8)
        nib[..., 0::2] = words & 0xF
        nib[..., 1::2] = words >> 4
        vals = E2M1[nib]
    vals = vals * np.repeat(np.exp2(scales.astype(np.float64) - 127.0), 8, axis=1)[..., None]
    return vals.transpose(0, 1, 3, 2).reshape(g * 512, n)


K, T, J, N = 1024, 1024, 256, 256


def setup_inputs():
    n = np.random.standard_normal
    idx = np.random.permutation(T)[:J]
    fk = mx_kscale(K)
    xtp = pack_weight(n((K, T)) * np.random.uniform(0.4, 1.6, (1, T)) / fk[:, None], "e5m2")
    wap = pack_weight(n((K, N)) * 1 / np.sqrt(K) * fk[:, None], "e5m2")
    return {
        "xt_words": xtp[0],
        "xt_scales": xtp[1],
        "wa_words": wap[0],
        "wa_scales": wap[1],
        "wb": (n((K, N)) * 1 / np.sqrt(K) * fk[:, None]).astype(np.float32),
        "bi": (np.random.uniform(-0.6, 0.6, (1, N))).astype(np.float32),
        "gm": (np.random.uniform(0.5, 2.0, (1, N))).astype(np.float32),
        "offs": striped(idx),
    }


def reference(xt_words, xt_scales, wa_words, wa_scales, wb, bi, gm, offs):
    idx = unstriped(offs)
    xtu = unpack_weight(xt_words, xt_scales, "e5m2")
    wau = unpack_weight(wa_words, wa_scales, "e5m2")
    xtidxg = xtu[:, idx]
    a = xtidxg.T @ wau
    wbq = mxq(f64(wb), 0, "e4m3")
    b0 = xtidxg.T @ wbq
    b2 = b0 + f64(bi)
    mb = np.mean(np.abs(b2), axis=1, keepdims=True)
    y = np.maximum(a - mb, 0.0) * f64(gm)
    return y

@@ -1,0 +1,136 @@
+from contextlib import ExitStack
+
+import concourse.mybir as mybir
+from concourse.masks import make_identity
+
+K, T, J, N = 1024, 1024, 256, 256
+FLOPS = 2 * 2 * K * J * N
+
+F32 = mybir.dt.float32
+BF16 = mybir.dt.bfloat16
+I32 = mybir.dt.int32
+U32 = mybir.dt.uint32
+U16 = mybir.dt.uint16
+U8 = mybir.dt.uint8
+E4X4 = mybir.dt.float8_e4m3fn_x4
+E5X4 = mybir.dt.float8_e5m2_x4
+ALU = mybir.AluOpType
+ACT = mybir.ActivationFunctionType
+
+P = 128
+PACK = 4
+PASSES = K // (P * PACK)
+TILES = J // P
+ROWS = 4
+
+
+def tile_list_rows_onetoken_abovemean_kernel(tc, xt_words, xt_scales, wa_words, wa_scales, wb, bi, gm, offs, out):
+    nc = tc.nc
+    with ExitStack() as ctx:
+        keep = ctx.enter_context(tc.tile_pool(name="keep", bufs=1))
+        psum = ctx.enter_context(tc.psum_pool(name="psum", bufs=1))
+
+        offsets = keep.tile([P, J // 16], U16, name="offsets")
+        nc.sync.dma_start(offsets[:], offs)
+
+        xs_all = keep.tile([P, PASSES, T], U8, name="xs_all", align_bytes=64)
+        nc.vector.memset(xs_all[:].bitcast(I32), 0)
+        was = keep.tile([P, PASSES, N], U8, name="was", align_bytes=64)
+        nc.vector.memset(was[:].bitcast(I32), 0)
+
+        wb_raw = [keep.tile([P, PACK, N], F32, name="wb_raw%d" % z) for z in range(PASSES)]
+        x_all = [keep.tile([P, T], U32, name="x_all%d" % z, align_bytes=64) for z in range(PASSES)]
+        waw = keep.tile([P, PASSES, N], U32, name="waw", align_bytes=64)
+        for z in range(PASSES):
+            nc.sync.dma_start(wb_raw[z][:], wb[z * P * PACK : (z + 1) * P * PACK, :].rearrange("(p t) n -> p t n", t=PACK))
+        xs_rows = xt_scales.rearrange("z (q r) c -> r q z c", r=ROWS)
+        for r in range(ROWS):
+            nc.scalar.dma_start(xs_all[r:P:32].bitcast(I32), xs_rows[r].bitcast(I32))
+        for z in range(PASSES):
+            nc.sync.dma_start(x_all[z][:].bitcast(I32), xt_words[z].rearrange("p c t -> p (c t)").bitcast(I32))
+        nc.sync.dma_start(waw[:].bitcast(I32), wa_words.rearrange("z p n t -> p z (n t)").bitcast(I32))
+
+        ident = keep.tile([P, P], F32, name="ident")
+        make_identity(nc, ident[:])
+        bi_col = keep.tile([P, 2], F32, name="bi_col")
+        gm_col = keep.tile([P, 2], F32, name="gm_col")
+        nc.gpsimd.dma_start(bi_col[:], bi.rearrange("o (p c) -> (o p) c", c=2))
+        nc.gpsimd.dma_start(gm_col[:], gm.rearrange("o (p c) -> (o p) c", c=2))
+        was_rows = wa_scales.rearrange("z (q r) n -> r q z n", r=ROWS)
+        for r in range(ROWS):
+            nc.gpsimd.dma_start(was[r:P:32].bitcast(I32), was_rows[r].bitcast(I32))
+
+        bi_ps = psum.tile([P, 2, P], F32, name="bi_ps")
+        gm_ps = psum.tile([P, 2, P], F32, name="gm_ps")
+        for c in range(2):
+            nc.tensor.transpose(bi_ps[:, c, :], bi_col[:, c : c + 1].to_broadcast([P, P]), ident[:])
+        for c in range(2):
+            nc.tensor.transpose(gm_ps[:, c, :], gm_col[:, c : c + 1].to_broadcast([P, P]), ident[:])
+        bias = keep.tile([P, P, 2], F32, name="bias")
+        nc.scalar.activation(bias[:], bi_ps[:].rearrange("m c p -> m p c"), ACT.Copy)
+
+        xs = [keep.tile([P, J], U8, name="xs%d" % z, align_bytes=64) for z in range(PASSES)]
+        for z in range(PASSES):
+            nc.vector.tensor_copy(xs[z][:], xs_all[:, z, :].indirect(offsets[:]))
+
+        grouped = [keep.tile([P, N, PACK], BF16, name="grouped%d" % z, align_bytes=64) for z in range(PASSES)]
+        wbq = [keep.tile([P, N], U32, name="wbq%d" % z, align_bytes=64) for z in range(PASSES)]
+        wbs = [keep.tile([P, N], U8, name="wbs%d" % z, align_bytes=64) for z in range(PASSES)]
+        for z, copy in enumerate((nc.scalar.copy, nc.vector.tensor_copy)):
+            copy(
+                grouped[z][:].rearrange("p (c i) t -> p c t i", i=4),
+                wb_raw[z][:].rearrange("p t (c i) -> p c t i", i=4),
+            )
+        for z in range(PASSES):
+            nc.vector.quantize_mx(
+                out=wbq[z][:].bitcast(E4X4), scales=wbs[z][:], in_=grouped[z][:].rearrange("p n t -> p (n t)")
+            )
+
+        x0 = keep.tile([P, J], U32, name="x0", align_bytes=64)
+        nc.vector.tensor_copy(x0[:], x_all[0][:].indirect(offsets[:]))
+        x1 = [keep.tile([P, P], U32, name="x1_%d" % j, align_bytes=64) for j in range(TILES)]
+        for j in range(TILES):
+            nc.vector.tensor_copy(x1[j][:], x_all[1][:].indirect(offsets[:, 8 * j : 8 * (j + 1)]))
+        xw = [[x0[:, j * P : (j + 1) * P] for j in range(TILES)], [x1[j][:] for j in range(TILES)]]
+
+        b_ps = [psum.tile([P, N], F32, name="b_ps%d" % j) for j in range(TILES)]
+        a_ps = [psum.tile([P, N], F32, name="a_ps%d" % j) for j in range(TILES)]
+        for z in range(PASSES):
+            for j in range(TILES):
+                nc.tensor.matmul_mx(
+                    out=b_ps[j][:],
+                    lhsT=xw[z][j].bitcast(E5X4),
+                    lhsT_scale=xs[z][:, j * P : (j + 1) * P],
+                    rhs=wbq[z][:].bitcast(E4X4),
+                    rhs_scale=wbs[z][:],
+                    start=(z == 0),
+                    stop=(z == PASSES - 1),
+                )
+        for j in range(TILES):
+            for z in range(PASSES):
+                nc.tensor.matmul_mx(
+                    out=a_ps[j][:],
+                    lhsT=xw[z][j].bitcast(E5X4),
+                    lhsT_scale=xs[z][:, j * P : (j + 1) * P],
+                    rhs=waw[:, z, :].bitcast(E5X4),
+                    rhs_scale=was[:, z, :],
+                    start=(z == 0),
+                    stop=(z == PASSES - 1),
+                )
+
+        b2 = [keep.tile([P, N], F32, name="b2_%d" % j) for j in range(TILES)]
+        mb = [keep.tile([P, 1], F32, name="mb%d" % j) for j in range(TILES)]
+        above = [keep.tile([P, N], F32, name="above%d" % j) for j in range(TILES)]
+        y = [keep.tile([P, N], F32, name="y%d" % j) for j in range(TILES)]
+        for j in range(TILES):
+            nc.vector.tensor_tensor(b2[j][:], b_ps[j][:], bias[:].rearrange("m p c -> m (p c)"), ALU.add)
+            nc.scalar.activation(b2[j][:], b2[j][:], ACT.Abs, scale=1.0 / N, accum_out=mb[j][:])
+        for j, queue in enumerate((nc.scalar, nc.sync)):
+            nc.vector.tensor_scalar(above[j][:], a_ps[j][:], mb[j][:], 0.0, ALU.subtract, ALU.max)
+            nc.vector.tensor_tensor(
+                y[j][:].rearrange("m (p c) -> m p c", c=2),
+                above[j][:].rearrange("m (p c) -> m p c", c=2),
+                gm_ps[:].rearrange("m c p -> m p c"),
+                ALU.mult,
+            )
+            queue.dma_start(out[j * P : (j + 1) * P, :], y[j][:])

@@ -34,31 +34,35 @@ def tile_list_rows_onetoken_abovemean_kernel(tc, xt_words, xt_scales, wa_words, 
         nc.sync.dma_start(offsets[:], offs)
 
         xs_all = keep.tile([P, PASSES, T], U8, name="xs_all", align_bytes=64)
-        nc.vector.memset(xs_all[:].bitcast(I32), 0)
+        nc.gpsimd.memset(xs_all[:].bitcast(I32), 0)
         was = keep.tile([P, PASSES, N], U8, name="was", align_bytes=64)
         nc.vector.memset(was[:].bitcast(I32), 0)
 
         wb_raw = [keep.tile([P, PACK, N], F32, name="wb_raw%d" % z) for z in range(PASSES)]
         x_all = [keep.tile([P, T], U32, name="x_all%d" % z, align_bytes=64) for z in range(PASSES)]
-        waw = keep.tile([P, PASSES, N], U32, name="waw", align_bytes=64)
-        for z in range(PASSES):
-            nc.sync.dma_start(wb_raw[z][:], wb[z * P * PACK : (z + 1) * P * PACK, :].rearrange("(p t) n -> p t n", t=PACK))
+        waw = [keep.tile([P, N], U32, name="waw%d" % z, align_bytes=64) for z in range(PASSES)]
+        bi_col = keep.tile([P, 2], F32, name="bi_col")
+        gm_col = keep.tile([P, 2], F32, name="gm_col")
+        wb_rows = wb.rearrange("(z p t) n -> z p t n", p=P, t=PACK)
         xs_rows = xt_scales.rearrange("z (q r) c -> r q z c", r=ROWS)
+        was_rows = wa_scales.rearrange("z (q r) n -> r q z n", r=ROWS)
+        nc.sync.dma_start(wb_raw[0][:], wb_rows[0])
+        nc.sync.dma_start(bi_col[:], bi.rearrange("o (p c) -> (o p) c", c=2))
+        nc.sync.dma_start(gm_col[:], gm.rearrange("o (p c) -> (o p) c", c=2))
         for r in range(ROWS):
-            nc.scalar.dma_start(xs_all[r:P:32].bitcast(I32), xs_rows[r].bitcast(I32))
-        for z in range(PASSES):
-            nc.sync.dma_start(x_all[z][:].bitcast(I32), xt_words[z].rearrange("p c t -> p (c t)").bitcast(I32))
-        nc.sync.dma_start(waw[:].bitcast(I32), wa_words.rearrange("z p n t -> p z (n t)").bitcast(I32))
+            nc.sync.dma_start(xs_all[r:P:32].bitcast(I32), xs_rows[r].bitcast(I32))
+        x_rows = xt_words.rearrange("z p c t -> z p (c t)").bitcast(I32)
+        wa_rows = wa_words.rearrange("z p n t -> z p (n t)").bitcast(I32)
+        nc.sync.dma_start(x_all[0][:].bitcast(I32), x_rows[0])
+        nc.sync.dma_start(wb_raw[1][:], wb_rows[1])
+        for r in range(ROWS):
+            nc.sync.dma_start(was[r:P:32].bitcast(I32), was_rows[r].bitcast(I32))
+        nc.sync.dma_start(waw[0][:].bitcast(I32), wa_rows[0])
+        nc.sync.dma_start(x_all[1][:].bitcast(I32), x_rows[1])
+        nc.sync.dma_start(waw[1][:].bitcast(I32), wa_rows[1])
 
         ident = keep.tile([P, P], F32, name="ident")
         make_identity(nc, ident[:])
-        bi_col = keep.tile([P, 2], F32, name="bi_col")
-        gm_col = keep.tile([P, 2], F32, name="gm_col")
-        nc.gpsimd.dma_start(bi_col[:], bi.rearrange("o (p c) -> (o p) c", c=2))
-        nc.gpsimd.dma_start(gm_col[:], gm.rearrange("o (p c) -> (o p) c", c=2))
-        was_rows = wa_scales.rearrange("z (q r) n -> r q z n", r=ROWS)
-        for r in range(ROWS):
-            nc.gpsimd.dma_start(was[r:P:32].bitcast(I32), was_rows[r].bitcast(I32))
 
         bi_ps = psum.tile([P, 2, P], F32, name="bi_ps")
         gm_ps = psum.tile([P, 2, P], F32, name="gm_ps")
@@ -66,57 +70,55 @@ def tile_list_rows_onetoken_abovemean_kernel(tc, xt_words, xt_scales, wa_words, 
             nc.tensor.transpose(bi_ps[:, c, :], bi_col[:, c : c + 1].to_broadcast([P, P]), ident[:])
         for c in range(2):
             nc.tensor.transpose(gm_ps[:, c, :], gm_col[:, c : c + 1].to_broadcast([P, P]), ident[:])
-        bias = keep.tile([P, P, 2], F32, name="bias")
-        nc.scalar.activation(bias[:], bi_ps[:].rearrange("m c p -> m p c"), ACT.Copy)
-
-        xs = [keep.tile([P, J], U8, name="xs%d" % z, align_bytes=64) for z in range(PASSES)]
-        for z in range(PASSES):
-            nc.vector.tensor_copy(xs[z][:], xs_all[:, z, :].indirect(offsets[:]))
 
         grouped = [keep.tile([P, N, PACK], BF16, name="grouped%d" % z, align_bytes=64) for z in range(PASSES)]
         wbq = [keep.tile([P, N], U32, name="wbq%d" % z, align_bytes=64) for z in range(PASSES)]
         wbs = [keep.tile([P, N], U8, name="wbs%d" % z, align_bytes=64) for z in range(PASSES)]
-        for z, copy in enumerate((nc.scalar.copy, nc.vector.tensor_copy)):
+        xs = [keep.tile([P, J], U8, name="xs%d" % z, align_bytes=64) for z in range(PASSES)]
+        x0 = keep.tile([P, J], U32, name="x0", align_bytes=64)
+        x1 = [keep.tile([P, P], U32, name="x1_%d" % j, align_bytes=64) for j in range(TILES)]
+        xw = [[x0[:, j * P : (j + 1) * P] for j in range(TILES)], [x1[j][:] for j in range(TILES)]]
+        bias = keep.tile([P, P, 2], F32, name="bias")
+
+        def round_wb(copy, z):
             copy(
                 grouped[z][:].rearrange("p (c i) t -> p c t i", i=4),
                 wb_raw[z][:].rearrange("p t (c i) -> p c t i", i=4),
             )
-        for z in range(PASSES):
+
+        def quantize_wb(z):
             nc.vector.quantize_mx(
                 out=wbq[z][:].bitcast(E4X4), scales=wbs[z][:], in_=grouped[z][:].rearrange("p n t -> p (n t)")
             )
 
-        x0 = keep.tile([P, J], U32, name="x0", align_bytes=64)
+        round_wb(nc.scalar.copy, 0)
+        nc.scalar.activation(bias[:], bi_ps[:].rearrange("m c p -> m p c"), ACT.Copy)
+        for z in range(PASSES):
+            nc.vector.tensor_copy(xs[z][:], xs_all[:, z, :].indirect(offsets[:]))
+        quantize_wb(0)
         nc.vector.tensor_copy(x0[:], x_all[0][:].indirect(offsets[:]))
-        x1 = [keep.tile([P, P], U32, name="x1_%d" % j, align_bytes=64) for j in range(TILES)]
+        round_wb(nc.vector.tensor_copy, 1)
+        quantize_wb(1)
         for j in range(TILES):
             nc.vector.tensor_copy(x1[j][:], x_all[1][:].indirect(offsets[:, 8 * j : 8 * (j + 1)]))
-        xw = [[x0[:, j * P : (j + 1) * P] for j in range(TILES)], [x1[j][:] for j in range(TILES)]]
 
         b_ps = [psum.tile([P, N], F32, name="b_ps%d" % j) for j in range(TILES)]
         a_ps = [psum.tile([P, N], F32, name="a_ps%d" % j) for j in range(TILES)]
         for z in range(PASSES):
-            for j in range(TILES):
-                nc.tensor.matmul_mx(
-                    out=b_ps[j][:],
-                    lhsT=xw[z][j].bitcast(E5X4),
-                    lhsT_scale=xs[z][:, j * P : (j + 1) * P],
-                    rhs=wbq[z][:].bitcast(E4X4),
-                    rhs_scale=wbs[z][:],
-                    start=(z == 0),
-                    stop=(z == PASSES - 1),
-                )
-        for j in range(TILES):
-            for z in range(PASSES):
-                nc.tensor.matmul_mx(
-                    out=a_ps[j][:],
-                    lhsT=xw[z][j].bitcast(E5X4),
-                    lhsT_scale=xs[z][:, j * P : (j + 1) * P],
-                    rhs=waw[:, z, :].bitcast(E5X4),
-                    rhs_scale=was[:, z, :],
-                    start=(z == 0),
-                    stop=(z == PASSES - 1),
-                )
+            for acc, words, scales in (
+                (b_ps, wbq[z][:].bitcast(E4X4), wbs[z][:]),
+                (a_ps, waw[z][:].bitcast(E5X4), was[:, z, :]),
+            ):
+                for j in range(TILES):
+                    nc.tensor.matmul_mx(
+                        out=acc[j][:],
+                        lhsT=xw[z][j].bitcast(E5X4),
+                        lhsT_scale=xs[z][:, j * P : (j + 1) * P],
+                        rhs=words,
+                        rhs_scale=scales,
+                        start=(z == 0),
+                        stop=(z == PASSES - 1),
+                    )
 
         b2 = [keep.tile([P, N], F32, name="b2_%d" % j) for j in range(TILES)]
         mb = [keep.tile([P, 1], F32, name="mb%d" % j) for j in range(TILES)]

@@ -35,39 +35,39 @@ def tile_list_rows_onetoken_abovemean_kernel(tc, xt_words, xt_scales, wa_words, 
 
         xs_all = keep.tile([P, PASSES, T], U8, name="xs_all", align_bytes=64)
         nc.gpsimd.memset(xs_all[:].bitcast(I32), 0)
+        ident = keep.tile([P, P], F32, name="ident")
+        nc.vector.memset(ident[:], 0.0)
         was = keep.tile([P, PASSES, N], U8, name="was", align_bytes=64)
         nc.vector.memset(was[:].bitcast(I32), 0)
 
         wb_raw = [keep.tile([P, PACK, N], F32, name="wb_raw%d" % z) for z in range(PASSES)]
         x_all = [keep.tile([P, T], U32, name="x_all%d" % z, align_bytes=64) for z in range(PASSES)]
-        waw = [keep.tile([P, N], U32, name="waw%d" % z, align_bytes=64) for z in range(PASSES)]
+        waw = keep.tile([P, PASSES, N], U32, name="waw", align_bytes=64)
         bi_col = keep.tile([P, 2], F32, name="bi_col")
         gm_col = keep.tile([P, 2], F32, name="gm_col")
         wb_rows = wb.rearrange("(z p t) n -> z p t n", p=P, t=PACK)
         xs_rows = xt_scales.rearrange("z (q r) c -> r q z c", r=ROWS)
         was_rows = wa_scales.rearrange("z (q r) n -> r q z n", r=ROWS)
+        x_rows = xt_words.rearrange("z p c t -> z p (c t)").bitcast(I32)
         nc.sync.dma_start(wb_raw[0][:], wb_rows[0])
         nc.sync.dma_start(bi_col[:], bi.rearrange("o (p c) -> (o p) c", c=2))
-        nc.sync.dma_start(gm_col[:], gm.rearrange("o (p c) -> (o p) c", c=2))
         for r in range(ROWS):
             nc.sync.dma_start(xs_all[r:P:32].bitcast(I32), xs_rows[r].bitcast(I32))
-        x_rows = xt_words.rearrange("z p c t -> z p (c t)").bitcast(I32)
-        wa_rows = wa_words.rearrange("z p n t -> z p (n t)").bitcast(I32)
-        nc.sync.dma_start(x_all[0][:].bitcast(I32), x_rows[0])
         nc.sync.dma_start(wb_raw[1][:], wb_rows[1])
+        nc.sync.dma_start(x_all[0][:].bitcast(I32), x_rows[0])
+        nc.sync.dma_start(gm_col[:], gm.rearrange("o (p c) -> (o p) c", c=2))
         for r in range(ROWS):
             nc.sync.dma_start(was[r:P:32].bitcast(I32), was_rows[r].bitcast(I32))
-        nc.sync.dma_start(waw[0][:].bitcast(I32), wa_rows[0])
         nc.sync.dma_start(x_all[1][:].bitcast(I32), x_rows[1])
-        nc.sync.dma_start(waw[1][:].bitcast(I32), wa_rows[1])
+        nc.sync.dma_start(waw[:].bitcast(I32), wa_words.rearrange("z p n t -> p z (n t)").bitcast(I32))
 
-        ident = keep.tile([P, P], F32, name="ident")
-        make_identity(nc, ident[:])
-
-        bi_ps = psum.tile([P, 2, P], F32, name="bi_ps")
-        gm_ps = psum.tile([P, 2, P], F32, name="gm_ps")
+        make_identity(nc, ident[:], nomemset=True)
+        bias = keep.tile([P, 2, P], F32, name="bias")
         for c in range(2):
-            nc.tensor.transpose(bi_ps[:, c, :], bi_col[:, c : c + 1].to_broadcast([P, P]), ident[:])
+            bi_ps = psum.tile([P, P], F32, name="bi_ps%d" % c, tag="b%d" % c)
+            nc.tensor.transpose(bi_ps[:], bi_col[:, c : c + 1].to_broadcast([P, P]), ident[:])
+            nc.scalar.copy(bias[:, c, :], bi_ps[:])
+        gm_ps = psum.tile([P, 2, P], F32, name="gm_ps")
         for c in range(2):
             nc.tensor.transpose(gm_ps[:, c, :], gm_col[:, c : c + 1].to_broadcast([P, P]), ident[:])
 
@@ -78,7 +78,6 @@ def tile_list_rows_onetoken_abovemean_kernel(tc, xt_words, xt_scales, wa_words, 
         x0 = keep.tile([P, J], U32, name="x0", align_bytes=64)
         x1 = [keep.tile([P, P], U32, name="x1_%d" % j, align_bytes=64) for j in range(TILES)]
         xw = [[x0[:, j * P : (j + 1) * P] for j in range(TILES)], [x1[j][:] for j in range(TILES)]]
-        bias = keep.tile([P, P, 2], F32, name="bias")
 
         def round_wb(copy, z):
             copy(
@@ -91,41 +90,48 @@ def tile_list_rows_onetoken_abovemean_kernel(tc, xt_words, xt_scales, wa_words, 
                 out=wbq[z][:].bitcast(E4X4), scales=wbs[z][:], in_=grouped[z][:].rearrange("p n t -> p (n t)")
             )
 
-        round_wb(nc.scalar.copy, 0)
-        nc.scalar.activation(bias[:], bi_ps[:].rearrange("m c p -> m p c"), ACT.Copy)
+        round_wb(nc.vector.tensor_copy, 0)
         for z in range(PASSES):
             nc.vector.tensor_copy(xs[z][:], xs_all[:, z, :].indirect(offsets[:]))
         quantize_wb(0)
-        nc.vector.tensor_copy(x0[:], x_all[0][:].indirect(offsets[:]))
-        round_wb(nc.vector.tensor_copy, 1)
+        round_wb(nc.scalar.copy, 1)
         quantize_wb(1)
+        nc.vector.tensor_copy(x0[:], x_all[0][:].indirect(offsets[:]))
         for j in range(TILES):
             nc.vector.tensor_copy(x1[j][:], x_all[1][:].indirect(offsets[:, 8 * j : 8 * (j + 1)]))
 
-        b_ps = [psum.tile([P, N], F32, name="b_ps%d" % j) for j in range(TILES)]
+        b_ps = [psum.tile([P, N], F32, name="b_ps%d" % j, tag="b%d" % j) for j in range(TILES)]
         a_ps = [psum.tile([P, N], F32, name="a_ps%d" % j) for j in range(TILES)]
+
+        def product(acc, z, j, words, scales, first):
+            nc.tensor.matmul_mx(
+                out=acc[:],
+                lhsT=xw[z][j].bitcast(E5X4),
+                lhsT_scale=xs[z][:, j * P : (j + 1) * P],
+                rhs=words,
+                rhs_scale=scales,
+                start=first,
+                stop=not first,
+            )
+
         for z in range(PASSES):
-            for acc, words, scales in (
-                (b_ps, wbq[z][:].bitcast(E4X4), wbs[z][:]),
-                (a_ps, waw[z][:].bitcast(E5X4), was[:, z, :]),
-            ):
-                for j in range(TILES):
-                    nc.tensor.matmul_mx(
-                        out=acc[j][:],
-                        lhsT=xw[z][j].bitcast(E5X4),
-                        lhsT_scale=xs[z][:, j * P : (j + 1) * P],
-                        rhs=words,
-                        rhs_scale=scales,
-                        start=(z == 0),
-                        stop=(z == PASSES - 1),
-                    )
+            for j in range(TILES):
+                product(b_ps[j], z, j, wbq[z][:].bitcast(E4X4), wbs[z][:], z == 0)
+        for j in range(TILES):
+            for z in (1, 0):
+                product(a_ps[j], z, j, waw[:, z, :].bitcast(E5X4), was[:, z, :], z == 1)
 
         b2 = [keep.tile([P, N], F32, name="b2_%d" % j) for j in range(TILES)]
         mb = [keep.tile([P, 1], F32, name="mb%d" % j) for j in range(TILES)]
         above = [keep.tile([P, N], F32, name="above%d" % j) for j in range(TILES)]
         y = [keep.tile([P, N], F32, name="y%d" % j) for j in range(TILES)]
         for j in range(TILES):
-            nc.vector.tensor_tensor(b2[j][:], b_ps[j][:], bias[:].rearrange("m p c -> m (p c)"), ALU.add)
+            nc.vector.tensor_tensor(
+                b2[j][:].rearrange("m (p c) -> m p c", c=2),
+                b_ps[j][:].rearrange("m (p c) -> m p c", c=2),
+                bias[:].rearrange("m c p -> m p c"),
+                ALU.add,
+            )
             nc.scalar.activation(b2[j][:], b2[j][:], ACT.Abs, scale=1.0 / N, accum_out=mb[j][:])
         for j, queue in enumerate((nc.scalar, nc.sync)):
             nc.vector.tensor_scalar(above[j][:], a_ps[j][:], mb[j][:], 0.0, ALU.subtract, ALU.max)

@@ -34,11 +34,10 @@ def tile_list_rows_onetoken_abovemean_kernel(tc, xt_words, xt_scales, wa_words, 
         nc.sync.dma_start(offsets[:], offs)
 
         xs_all = keep.tile([P, PASSES, T], U8, name="xs_all", align_bytes=64)
-        nc.gpsimd.memset(xs_all[:].bitcast(I32), 0)
+        nc.vector.memset(xs_all[:].bitcast(I32), 0)
         ident = keep.tile([P, P], F32, name="ident")
-        nc.vector.memset(ident[:], 0.0)
         was = keep.tile([P, PASSES, N], U8, name="was", align_bytes=64)
-        nc.vector.memset(was[:].bitcast(I32), 0)
+        nc.gpsimd.memset(was[:].bitcast(I32), 0)
 
         wb_raw = [keep.tile([P, PACK, N], F32, name="wb_raw%d" % z) for z in range(PASSES)]
         x_all = [keep.tile([P, T], U32, name="x_all%d" % z, align_bytes=64) for z in range(PASSES)]
@@ -56,12 +55,12 @@ def tile_list_rows_onetoken_abovemean_kernel(tc, xt_words, xt_scales, wa_words, 
         nc.sync.dma_start(wb_raw[1][:], wb_rows[1])
         nc.sync.dma_start(x_all[0][:].bitcast(I32), x_rows[0])
         nc.sync.dma_start(gm_col[:], gm.rearrange("o (p c) -> (o p) c", c=2))
+        nc.sync.dma_start(x_all[1][:].bitcast(I32), x_rows[1])
         for r in range(ROWS):
             nc.sync.dma_start(was[r:P:32].bitcast(I32), was_rows[r].bitcast(I32))
-        nc.sync.dma_start(x_all[1][:].bitcast(I32), x_rows[1])
         nc.sync.dma_start(waw[:].bitcast(I32), wa_words.rearrange("z p n t -> p z (n t)").bitcast(I32))
 
-        make_identity(nc, ident[:], nomemset=True)
+        make_identity(nc, ident[:])
         bias = keep.tile([P, 2, P], F32, name="bias")
         for c in range(2):
             bi_ps = psum.tile([P, P], F32, name="bi_ps%d" % c, tag="b%d" % c)
@@ -95,8 +94,8 @@ def tile_list_rows_onetoken_abovemean_kernel(tc, xt_words, xt_scales, wa_words, 
             nc.vector.tensor_copy(xs[z][:], xs_all[:, z, :].indirect(offsets[:]))
         quantize_wb(0)
         round_wb(nc.scalar.copy, 1)
-        quantize_wb(1)
         nc.vector.tensor_copy(x0[:], x_all[0][:].indirect(offsets[:]))
+        quantize_wb(1)
         for j in range(TILES):
             nc.vector.tensor_copy(x1[j][:], x_all[1][:].indirect(offsets[:, 8 * j : 8 * (j + 1)]))
 
@@ -123,6 +122,7 @@ def tile_list_rows_onetoken_abovemean_kernel(tc, xt_words, xt_scales, wa_words, 
 
         b2 = [keep.tile([P, N], F32, name="b2_%d" % j) for j in range(TILES)]
         mb = [keep.tile([P, 1], F32, name="mb%d" % j) for j in range(TILES)]
+        minus_mb1 = keep.tile([P, 1], F32, name="minus_mb1")
         above = [keep.tile([P, N], F32, name="above%d" % j) for j in range(TILES)]
         y = [keep.tile([P, N], F32, name="y%d" % j) for j in range(TILES)]
         for j in range(TILES):
@@ -133,12 +133,14 @@ def tile_list_rows_onetoken_abovemean_kernel(tc, xt_words, xt_scales, wa_words, 
                 ALU.add,
             )
             nc.scalar.activation(b2[j][:], b2[j][:], ACT.Abs, scale=1.0 / N, accum_out=mb[j][:])
-        for j, queue in enumerate((nc.scalar, nc.sync)):
-            nc.vector.tensor_scalar(above[j][:], a_ps[j][:], mb[j][:], 0.0, ALU.subtract, ALU.max)
+        nc.vector.tensor_scalar(above[0][:], a_ps[0][:], mb[0][:], 0.0, ALU.subtract, ALU.max)
+        nc.scalar.activation(minus_mb1[:], mb[1][:], ACT.Copy, scale=-1.0)
+        nc.scalar.activation(above[1][:], a_ps[1][:], ACT.Relu, bias=minus_mb1[:])
+        for j in range(TILES):
             nc.vector.tensor_tensor(
                 y[j][:].rearrange("m (p c) -> m p c", c=2),
                 above[j][:].rearrange("m (p c) -> m p c", c=2),
                 gm_ps[:].rearrange("m c p -> m p c"),
                 ALU.mult,
             )
-            queue.dma_start(out[j * P : (j + 1) * P, :], y[j][:])
+            nc.sync.dma_start(out[j * P : (j + 1) * P, :], y[j][:])

from contextlib import ExitStack

import concourse.mybir as mybir
from concourse.masks import make_identity

K, T, J, N = 1024, 1024, 256, 256
FLOPS = 2 * 2 * K * J * N

F32 = mybir.dt.float32
BF16 = mybir.dt.bfloat16
I32 = mybir.dt.int32
U32 = mybir.dt.uint32
U16 = mybir.dt.uint16
U8 = mybir.dt.uint8
E4X4 = mybir.dt.float8_e4m3fn_x4
E5X4 = mybir.dt.float8_e5m2_x4
ALU = mybir.AluOpType
ACT = mybir.ActivationFunctionType

P = 128
PACK = 4
PASSES = K // (P * PACK)
TILES = J // P
ROWS = 4


def tile_list_rows_onetoken_abovemean_kernel(tc, xt_words, xt_scales, wa_words, wa_scales, wb, bi, gm, offs, out):
    nc = tc.nc
    with ExitStack() as ctx:
        keep = ctx.enter_context(tc.tile_pool(name="keep", bufs=1))
        psum = ctx.enter_context(tc.psum_pool(name="psum", bufs=1))

        offsets = keep.tile([P, J // 16], U16, name="offsets")
        nc.sync.dma_start(offsets[:], offs)

        xs_all = keep.tile([P, PASSES, T], U8, name="xs_all", align_bytes=64)
        nc.vector.memset(xs_all[:].bitcast(I32), 0)
        ident = keep.tile([P, P], F32, name="ident")
        was = keep.tile([P, PASSES, N], U8, name="was", align_bytes=64)
        nc.gpsimd.memset(was[:].bitcast(I32), 0)

        wb_raw = [keep.tile([P, PACK, N], F32, name="wb_raw%d" % z) for z in range(PASSES)]
        x_all = [keep.tile([P, T], U32, name="x_all%d" % z, align_bytes=64) for z in range(PASSES)]
        waw = keep.tile([P, PASSES, N], U32, name="waw", align_bytes=64)
        bi_col = keep.tile([P, 2], F32, name="bi_col")
        gm_col = keep.tile([P, 2], F32, name="gm_col")
        wb_rows = wb.rearrange("(z p t) n -> z p t n", p=P, t=PACK)
        xs_rows = xt_scales.rearrange("z (q r) c -> r q z c", r=ROWS)
        was_rows = wa_scales.rearrange("z (q r) n -> r q z n", r=ROWS)
        x_rows = xt_words.rearrange("z p c t -> z p (c t)").bitcast(I32)
        nc.sync.dma_start(wb_raw[0][:], wb_rows[0])
        nc.sync.dma_start(bi_col[:], bi.rearrange("o (p c) -> (o p) c", c=2))
        for r in range(ROWS):
            nc.sync.dma_start(xs_all[r:P:32].bitcast(I32), xs_rows[r].bitcast(I32))
        nc.sync.dma_start(wb_raw[1][:], wb_rows[1])
        nc.sync.dma_start(x_all[0][:].bitcast(I32), x_rows[0])
        nc.sync.dma_start(gm_col[:], gm.rearrange("o (p c) -> (o p) c", c=2))
        nc.sync.dma_start(x_all[1][:].bitcast(I32), x_rows[1])
        for r in range(ROWS):
            nc.sync.dma_start(was[r:P:32].bitcast(I32), was_rows[r].bitcast(I32))
        nc.sync.dma_start(waw[:].bitcast(I32), wa_words.rearrange("z p n t -> p z (n t)").bitcast(I32))

        make_identity(nc, ident[:])
        bias = keep.tile([P, 2, P], F32, name="bias")
        for c in range(2):
            bi_ps = psum.tile([P, P], F32, name="bi_ps%d" % c, tag="b%d" % c)
            nc.tensor.transpose(bi_ps[:], bi_col[:, c : c + 1].to_broadcast([P, P]), ident[:])
            nc.scalar.copy(bias[:, c, :], bi_ps[:])
        gm_ps = psum.tile([P, 2, P], F32, name="gm_ps")
        for c in range(2):
            nc.tensor.transpose(gm_ps[:, c, :], gm_col[:, c : c + 1].to_broadcast([P, P]), ident[:])

        grouped = [keep.tile([P, N, PACK], BF16, name="grouped%d" % z, align_bytes=64) for z in range(PASSES)]
        wbq = [keep.tile([P, N], U32, name="wbq%d" % z, align_bytes=64) for z in range(PASSES)]
        wbs = [keep.tile([P, N], U8, name="wbs%d" % z, align_bytes=64) for z in range(PASSES)]
        xs = [keep.tile([P, J], U8, name="xs%d" % z, align_bytes=64) for z in range(PASSES)]
        x0 = keep.tile([P, J], U32, name="x0", align_bytes=64)
        x1 = [keep.tile([P, P], U32, name="x1_%d" % j, align_bytes=64) for j in range(TILES)]
        xw = [[x0[:, j * P : (j + 1) * P] for j in range(TILES)], [x1[j][:] for j in range(TILES)]]

        def round_wb(copy, z):
            copy(
                grouped[z][:].rearrange("p (c i) t -> p c t i", i=4),
                wb_raw[z][:].rearrange("p t (c i) -> p c t i", i=4),
            )

        def quantize_wb(z):
            nc.vector.quantize_mx(
                out=wbq[z][:].bitcast(E4X4), scales=wbs[z][:], in_=grouped[z][:].rearrange("p n t -> p (n t)")
            )

        round_wb(nc.vector.tensor_copy, 0)
        for z in range(PASSES):
            nc.vector.tensor_copy(xs[z][:], xs_all[:, z, :].indirect(offsets[:]))
        quantize_wb(0)
        round_wb(nc.scalar.copy, 1)
        nc.vector.tensor_copy(x0[:], x_all[0][:].indirect(offsets[:]))
        quantize_wb(1)
        for j in range(TILES):
            nc.vector.tensor_copy(x1[j][:], x_all[1][:].indirect(offsets[:, 8 * j : 8 * (j + 1)]))

        b_ps = [psum.tile([P, N], F32, name="b_ps%d" % j, tag="b%d" % j) for j in range(TILES)]
        a_ps = [psum.tile([P, N], F32, name="a_ps%d" % j) for j in range(TILES)]

        def product(acc, z, j, words, scales, first):
            nc.tensor.matmul_mx(
                out=acc[:],
                lhsT=xw[z][j].bitcast(E5X4),
                lhsT_scale=xs[z][:, j * P : (j + 1) * P],
                rhs=words,
                rhs_scale=scales,
                start=first,
                stop=not first,
            )

        for z in range(PASSES):
            for j in range(TILES):
                product(b_ps[j], z, j, wbq[z][:].bitcast(E4X4), wbs[z][:], z == 0)
        for j in range(TILES):
            for z in (1, 0):
                product(a_ps[j], z, j, waw[:, z, :].bitcast(E5X4), was[:, z, :], z == 1)

        b2 = [keep.tile([P, N], F32, name="b2_%d" % j) for j in range(TILES)]
        mb = [keep.tile([P, 1], F32, name="mb%d" % j) for j in range(TILES)]
        minus_mb1 = keep.tile([P, 1], F32, name="minus_mb1")
        above = [keep.tile([P, N], F32, name="above%d" % j) for j in range(TILES)]
        y = [keep.tile([P, N], F32, name="y%d" % j) for j in range(TILES)]
        for j in range(TILES):
            nc.vector.tensor_tensor(
                b2[j][:].rearrange("m (p c) -> m p c", c=2),
                b_ps[j][:].rearrange("m (p c) -> m p c", c=2),
                bias[:].rearrange("m c p -> m p c"),
                ALU.add,
            )
            nc.scalar.activation(b2[j][:], b2[j][:], ACT.Abs, scale=1.0 / N, accum_out=mb[j][:])
        nc.vector.tensor_scalar(above[0][:], a_ps[0][:], mb[0][:], 0.0, ALU.subtract, ALU.max)
        nc.scalar.activation(minus_mb1[:], mb[1][:], ACT.Copy, scale=-1.0)
        nc.scalar.activation(above[1][:], a_ps[1][:], ACT.Relu, bias=minus_mb1[:])
        for j in range(TILES):
            nc.vector.tensor_tensor(
                y[j][:].rearrange("m (p c) -> m p c", c=2),
                above[j][:].rearrange("m (p c) -> m p c", c=2),
                gm_ps[:].rearrange("m c p -> m p c"),
                ALU.mult,
            )
            nc.sync.dma_start(out[j * P : (j + 1) * P, :], y[j][:])
